import numpy as np
CORES = [50,52,122,124]
N = 4
TIMES = 1
def setup_inputs(rng):
    x = (rng.standard_normal((N, 128, 128), dtype=np.float32) / np.float32(np.sqrt(512 * N)))
    return {"x": x, "xt": x.transpose(0, 2, 1).copy()}
def setup_inputs_big(rng):
    d = setup_inputs(rng)
    for k in ("x", "xt"): d[k] = (d[k].astype(np.float32) * 1024.0).astype(d[k].dtype)
    return d
def setup_inputs_small(rng):
    d = setup_inputs(rng)
    for k in ("x", "xt"): d[k] = (d[k].astype(np.float32) * (1 / 1024.0)).astype(d[k].dtype)
    return d
def setup_inputs_apart(rng):
    d = setup_inputs(rng)
    f = (10.0 ** rng.permutation(np.linspace(-1.5, 1.5, N))).astype(np.float32).reshape(N, 1, 1)
    for k in ("x", "xt"): d[k] = (d[k].astype(np.float32) * f).astype(d[k].dtype)
    return d
def reference(x, xt):
    X = list(x.astype(np.float64))
    for _ in range(TIMES):
        G = sum(a.T @ a for a in X)
        X = [1.5 * a - 0.5 * (a @ G) for a in X]
    return {"y": np.stack(X).astype(np.float32)}

@@ -1,0 +1,138 @@
+from concourse.bass import DstId, RemoteDMATransfer
+from concourse.mybir import AluOpType
+
+P = 128
+NR = 4
+
+SCRATCH = {
+    "xs": ("sbuf", [P, P], "float32"),
+    "xts": ("sbuf", [P, P], "float32"),
+    "px": ("sbuf", [P, NR * P], "float32"),
+    "hf": ("sbuf", [P, NR * P], "float32"),
+    "cm": ("sbuf", [P, P], "float32"),
+    "cp": ("sbuf", [P, P], "float32"),
+    "x15": ("sbuf", [P, P], "float32"),
+    "h": ("sbuf", [P, P], "float32"),
+    "ys": ("sbuf", [P, P], "float32"),
+    "pg": ("psum", [P, 512], "float32"),
+    "py": ("psum", [P, 512], "float32"),
+}
+SEMAPHORES = ["ldx", "ldxt", "cst", "x15", "peer", "gdone", "hdone", "far", "pdone", "ydone", "stored", "left"]
+
+
+def _engines(mask):
+    return [b for b in range(16) if (mask >> b) & 1]
+
+
+def _pick(engs, n):
+    step = max(1, len(engs) // n)
+    m = 0
+    for b in engs[::step][:n]:
+        m |= 1 << b
+    return m
+
+
+def _count(mask):
+    return len(_engines(mask))
+
+
+def _plan(core, T, topo):
+    cores = list(T.cores)
+    near = lambda c: [d for d in cores if d != c and topo.chip(d) == topo.chip(c)]
+    far = lambda c: [d for d in cores if topo.chip(d) != topo.chip(c)]
+
+    def gateway(ch):
+        for c in cores:
+            if topo.chip(c) == ch and all(topo.may_write(c, d) for d in far(c)):
+                return c
+        return None
+
+    return near, far, gateway
+
+
+def _near_mask(src, dst, T, topo):
+    near, far, gateway = _plan(src, T, topo)
+    on_chip = topo.mask(src, dst)
+    if gateway(topo.chip(src)) == src:
+        m = on_chip
+        for d in far(src):
+            m &= topo.mask(src, d)
+        return m
+    return _pick(_engines(on_chip), 8)
+
+
+def _far_mask(src, T, topo):
+    near, far, gateway = _plan(src, T, topo)
+    m = topo.mask(src, far(src)[0])
+    for d in far(src):
+        m &= topo.mask(src, d)
+    return m
+
+
+def rank_program(g, core, T, topo):
+    rank = T.rank_of(core)
+    if rank is None:
+        return
+    near, far, gateway = _plan(core, T, topo)
+    S = T.sem
+    slot = lambda buf, c: buf[:, T.rank_of(c) * P:(T.rank_of(c) + 1) * P]
+    my_near = near(core)
+    far_gates = sorted(set(gateway(topo.chip(d)) for d in far(core)))
+    i_am_gate = gateway(topo.chip(core)) == core
+    pg = T.pg[:, 0:P]
+    py = T.py[:, 0:P]
+
+    g.sync.dma_start(T.xs[:], T.x[:]).then_inc(S.ldx, 16)
+    g.sync.dma_start(T.xts[:], T.xt[:]).then_inc(S.ldxt, 16)
+
+    left = 0
+    g.wait_ge(S.ldx, 16)
+    for d in my_near:
+        rid, pid, _ = topo.addr(d)
+        m = _near_mask(core, d, T, topo)
+        g.remote_dma(slot(T.px, core), T.xs[:], S.peer, S.left, pid, rid, m)
+        left += _count(m)
+    if i_am_gate:
+        m = _far_mask(core, T, topo)
+        ids = []
+        for d in far(core):
+            rid, pid, _ = topo.addr(d)
+            ids.append(DstId(rid=rid, pnc=pid))
+        g.wait_ge(S.hdone, 1)
+        g.remote_dma_fused(
+            [RemoteDMATransfer(dst_ids=ids, dma_engine_mask=m, remote_sem=S.far,
+                               srcs=[T.h[:]], dsts=[slot(T.hf, core) for _ in ids])],
+            local_sem=S.left)
+        left += _count(m)
+    g.wait_ge(S.left, left)
+
+    t = g.tensor
+    t.wait_ge(S.ldx, 16)
+    t.matmul(pg, T.xs[:], T.xs[:], True, False)
+    t.wait_ge(S.peer, sum(_count(_near_mask(d, core, T, topo)) for d in my_near))
+    for i, d in enumerate(my_near):
+        mm = t.matmul(pg, slot(T.px, d), slot(T.px, d), False, i == len(my_near) - 1)
+    mm.then_inc(S.gdone, 1)
+    t.wait_ge(S.hdone, 1)
+    t.wait_ge(S.ldxt, 16)
+    t.matmul(py, T.xts[:], T.h[:], True, False)
+    t.wait_ge(S.far, sum(_count(_far_mask(c, T, topo)) for c in far_gates))
+    for i, c in enumerate(far_gates):
+        mm = t.matmul(py, T.xts[:], slot(T.hf, c), False, i == len(far_gates) - 1)
+    mm.then_inc(S.pdone, 1)
+
+    v = g.vector
+    v.memset(T.cm[:], -0.5).then_inc(S.cst, 1)
+    v.memset(T.cp[:], 1.5).then_inc(S.cst, 1)
+    v.wait_ge(S.cst, 2)
+    v.wait_ge(S.ldx, 16)
+    v.tensor_tensor(T.x15[:], T.xs[:], T.cp[:], AluOpType.mult).then_inc(S.x15, 1)
+    v.wait_ge(S.gdone, 1)
+    v.tensor_tensor(T.h[:], pg, T.cm[:], AluOpType.mult).then_inc(S.hdone, 1)
+    v.wait_ge(S.x15, 1)
+    v.wait_ge(S.pdone, 1)
+    v.tensor_tensor(T.ys[:], py, T.x15[:], AluOpType.add).then_inc(S.ydone, 1)
+
+    g.sync.wait_ge(S.ydone, 1)
+    g.sync.dma_start(T.y[:], T.ys[:]).then_inc(S.stored, 16)
+    g.sync.wait_ge(S.stored, 16)

@@ -3,25 +3,35 @@ from concourse.mybir import AluOpType
 
 P = 128
 NR = 4
+HB = P // 2
+BLK = ((0, HB), (HB, P))
 
 SCRATCH = {
     "xs": ("sbuf", [P, P], "float32"),
     "xts": ("sbuf", [P, P], "float32"),
+    "xd": ("dram", [P, P], "float32"),
     "px": ("sbuf", [P, NR * P], "float32"),
     "hf": ("sbuf", [P, NR * P], "float32"),
-    "cm": ("sbuf", [P, P], "float32"),
+    "cm": ("sbuf", [P, HB], "float32"),
     "cp": ("sbuf", [P, P], "float32"),
     "x15": ("sbuf", [P, P], "float32"),
     "h": ("sbuf", [P, P], "float32"),
     "ys": ("sbuf", [P, P], "float32"),
-    "pg": ("psum", [P, 512], "float32"),
-    "py": ("psum", [P, 512], "float32"),
+    "pg0": ("psum", [P, 512], "float32"),
+    "pg1": ("psum", [P, 512], "float32"),
+    "py0": ("psum", [P, 512], "float32"),
+    "py1": ("psum", [P, 512], "float32"),
 }
-SEMAPHORES = ["ldx", "ldxt", "cst", "x15", "peer", "gdone", "hdone", "far", "pdone", "ydone", "stored", "left"]
+SEMAPHORES = ["ldxd", "ldx", "ldxt", "cst", "x15", "peer", "g0", "g1", "h0", "h1", "far0", "far1",
+              "p0", "p1", "y0", "y1", "st0", "st1", "left"]
 
 
 def _engines(mask):
     return [b for b in range(16) if (mask >> b) & 1]
+
+
+def _count(mask):
+    return len(_engines(mask))
 
 
 def _pick(engs, n):
@@ -32,14 +42,14 @@ def _pick(engs, n):
     return m
 
 
-def _count(mask):
-    return len(_engines(mask))
-
-
-def _plan(core, T, topo):
+def _plan(T, topo):
     cores = list(T.cores)
-    near = lambda c: [d for d in cores if d != c and topo.chip(d) == topo.chip(c)]
-    far = lambda c: [d for d in cores if topo.chip(d) != topo.chip(c)]
+
+    def near(c):
+        return [d for d in cores if d != c and topo.chip(d) == topo.chip(c)]
+
+    def far(c):
+        return [d for d in cores if topo.chip(d) != topo.chip(c)]
 
     def gateway(ch):
         for c in cores:
@@ -47,79 +57,90 @@ def _plan(core, T, topo):
                 return c
         return None
 
-    return near, far, gateway
-
-
-def _near_mask(src, dst, T, topo):
-    near, far, gateway = _plan(src, T, topo)
-    on_chip = topo.mask(src, dst)
-    if gateway(topo.chip(src)) == src:
-        m = on_chip
-        for d in far(src):
-            m &= topo.mask(src, d)
+    def off_mask(c):
+        m = topo.mask(c, far(c)[0])
+        for d in far(c):
+            m &= topo.mask(c, d)
         return m
-    return _pick(_engines(on_chip), 8)
 
+    def x_mask(c):
+        on_chip = topo.mask(c, near(c)[0])
+        if gateway(topo.chip(c)) == c:
+            return on_chip
+        return _pick(_engines(on_chip), 8)
 
-def _far_mask(src, T, topo):
-    near, far, gateway = _plan(src, T, topo)
-    m = topo.mask(src, far(src)[0])
-    for d in far(src):
-        m &= topo.mask(src, d)
-    return m
+    return near, far, gateway, off_mask, x_mask
 
 
 def rank_program(g, core, T, topo):
-    rank = T.rank_of(core)
-    if rank is None:
+    if T.rank_of(core) is None:
         return
-    near, far, gateway = _plan(core, T, topo)
+    near, far, gateway, off_mask, x_mask = _plan(T, topo)
     S = T.sem
-    slot = lambda buf, c: buf[:, T.rank_of(c) * P:(T.rank_of(c) + 1) * P]
-    my_near = near(core)
-    far_gates = sorted(set(gateway(topo.chip(d)) for d in far(core)))
-    i_am_gate = gateway(topo.chip(core)) == core
-    pg = T.pg[:, 0:P]
-    py = T.py[:, 0:P]
+    nb = near(core)[0]
+    gate = gateway(topo.chip(core)) == core
+    fgate = gateway(topo.chip(far(core)[0]))
 
+    def cols(buf, c, b=None):
+        o = T.rank_of(c) * P
+        if b is None:
+            return buf[:, o:o + P]
+        return buf[:, o + BLK[b][0]:o + BLK[b][1]]
+
+    def blk(buf, b):
+        return buf[:, BLK[b][0]:BLK[b][1]]
+
+    pg = (T.pg0[:, 0:HB], T.pg1[:, 0:HB])
+    py = (T.py0[:, 0:HB], T.py1[:, 0:HB])
+    sg, sh, sfar = (S.g0, S.g1), (S.h0, S.h1), (S.far0, S.far1)
+    sp, sy, sst = (S.p0, S.p1), (S.y0, S.y1), (S.st0, S.st1)
+    n_far = _count(off_mask(fgate))
+
+    if not gate:
+        g.sync.dma_start(T.xd[:], T.x[:]).then_inc(S.ldxd, 16)
     g.sync.dma_start(T.xs[:], T.x[:]).then_inc(S.ldx, 16)
     g.sync.dma_start(T.xts[:], T.xt[:]).then_inc(S.ldxt, 16)
 
     left = 0
-    g.wait_ge(S.ldx, 16)
-    for d in my_near:
-        rid, pid, _ = topo.addr(d)
-        m = _near_mask(core, d, T, topo)
-        g.remote_dma(slot(T.px, core), T.xs[:], S.peer, S.left, pid, rid, m)
-        left += _count(m)
-    if i_am_gate:
-        m = _far_mask(core, T, topo)
-        ids = []
-        for d in far(core):
-            rid, pid, _ = topo.addr(d)
-            ids.append(DstId(rid=rid, pnc=pid))
-        g.wait_ge(S.hdone, 1)
-        g.remote_dma_fused(
-            [RemoteDMATransfer(dst_ids=ids, dma_engine_mask=m, remote_sem=S.far,
-                               srcs=[T.h[:]], dsts=[slot(T.hf, core) for _ in ids])],
-            local_sem=S.left)
-        left += _count(m)
+    nrid, npid, _ = topo.addr(nb)
+    m = x_mask(core)
+    if gate:
+        g.wait_ge(S.ldx, 16)
+        g.remote_dma(cols(T.px, core), T.xs[:], S.peer, S.left, npid, nrid, m)
+    else:
+        g.wait_ge(S.ldxd, 16)
+        g.remote_dma(cols(T.px, core), T.xd[:], S.peer, S.left, npid, nrid, m)
+    left += _count(m)
+    if gate:
+        mo = off_mask(core)
+        for b in (0, 1):
+            dsts = far(core) if b == 0 else far(core)[::-1]
+            ids = []
+            for d in dsts:
+                rid, pid, _ = topo.addr(d)
+                ids.append(DstId(rid=rid, pnc=pid))
+            g.wait_ge(sh[b], 1)
+            g.remote_dma_fused(
+                [RemoteDMATransfer(dst_ids=ids, dma_engine_mask=mo, remote_sem=sfar[b],
+                                   srcs=[blk(T.h, b)], dsts=[cols(T.hf, core, b) for _ in ids])],
+                local_sem=S.left)
+            left += _count(mo)
     g.wait_ge(S.left, left)
 
     t = g.tensor
     t.wait_ge(S.ldx, 16)
-    t.matmul(pg, T.xs[:], T.xs[:], True, False)
-    t.wait_ge(S.peer, sum(_count(_near_mask(d, core, T, topo)) for d in my_near))
-    for i, d in enumerate(my_near):
-        mm = t.matmul(pg, slot(T.px, d), slot(T.px, d), False, i == len(my_near) - 1)
-    mm.then_inc(S.gdone, 1)
-    t.wait_ge(S.hdone, 1)
+    for b in (0, 1):
+        t.matmul(pg[b], T.xs[:], blk(T.xs, b), True, False)
+    t.wait_ge(S.peer, _count(x_mask(nb)))
+    for b in (0, 1):
+        t.matmul(pg[b], cols(T.px, nb), cols(T.px, nb, b), False, True).then_inc(sg[b], 1)
     t.wait_ge(S.ldxt, 16)
-    t.matmul(py, T.xts[:], T.h[:], True, False)
-    t.wait_ge(S.far, sum(_count(_far_mask(c, T, topo)) for c in far_gates))
-    for i, c in enumerate(far_gates):
-        mm = t.matmul(py, T.xts[:], slot(T.hf, c), False, i == len(far_gates) - 1)
-    mm.then_inc(S.pdone, 1)
+    for b in (0, 1):
+        t.wait_ge(sh[b], 1)
+        t.matmul(py[b], T.xts[:], blk(T.h, b), True, False)
+    for b in (0, 1):
+        t.wait_ge(sfar[b], n_far)
+        t.matmul(py[b], T.xts[:], cols(T.hf, fgate, b), False, True).then_inc(sp[b], 1)
 
     v = g.vector
     v.memset(T.cm[:], -0.5).then_inc(S.cst, 1)
@@ -127,12 +148,15 @@ def rank_program(g, core, T, topo):
     v.wait_ge(S.cst, 2)
     v.wait_ge(S.ldx, 16)
     v.tensor_tensor(T.x15[:], T.xs[:], T.cp[:], AluOpType.mult).then_inc(S.x15, 1)
-    v.wait_ge(S.gdone, 1)
-    v.tensor_tensor(T.h[:], pg, T.cm[:], AluOpType.mult).then_inc(S.hdone, 1)
+    for b in (0, 1):
+        v.wait_ge(sg[b], 1)
+        v.tensor_tensor(blk(T.h, b), pg[b], T.cm[:], AluOpType.mult).then_inc(sh[b], 1)
     v.wait_ge(S.x15, 1)
-    v.wait_ge(S.pdone, 1)
-    v.tensor_tensor(T.ys[:], py, T.x15[:], AluOpType.add).then_inc(S.ydone, 1)
+    for b in (0, 1):
+        v.wait_ge(sp[b], 1)
+        v.tensor_tensor(blk(T.ys, b), py[b], blk(T.x15, b), AluOpType.add).then_inc(sy[b], 1)
 
-    g.sync.wait_ge(S.ydone, 1)
-    g.sync.dma_start(T.y[:], T.ys[:]).then_inc(S.stored, 16)
-    g.sync.wait_ge(S.stored, 16)
+    for q, b in ((g.scalar, 0), (g.sync, 1)):
+        q.wait_ge(sy[b], 1)
+        q.dma_start(blk(T.y, b), blk(T.ys, b)).then_inc(sst[b], 16)
+        q.wait_ge(sst[b], 16)

from concourse.bass import DstId, RemoteDMATransfer
from concourse.mybir import AluOpType

P = 128
NR = 4
HB = P // 2
BLK = ((0, HB), (HB, P))

SCRATCH = {
    "xs": ("sbuf", [P, P], "float32"),
    "xts": ("sbuf", [P, P], "float32"),
    "xd": ("dram", [P, P], "float32"),
    "px": ("sbuf", [P, NR * P], "float32"),
    "hf": ("sbuf", [P, NR * P], "float32"),
    "cm": ("sbuf", [P, HB], "float32"),
    "cp": ("sbuf", [P, P], "float32"),
    "x15": ("sbuf", [P, P], "float32"),
    "h": ("sbuf", [P, P], "float32"),
    "ys": ("sbuf", [P, P], "float32"),
    "pg0": ("psum", [P, 512], "float32"),
    "pg1": ("psum", [P, 512], "float32"),
    "py0": ("psum", [P, 512], "float32"),
    "py1": ("psum", [P, 512], "float32"),
}
SEMAPHORES = ["ldxd", "ldx", "ldxt", "cst", "x15", "peer", "g0", "g1", "h0", "h1", "far0", "far1",
              "p0", "p1", "y0", "y1", "st0", "st1", "left"]


def _engines(mask):
    return [b for b in range(16) if (mask >> b) & 1]


def _count(mask):
    return len(_engines(mask))


def _pick(engs, n):
    step = max(1, len(engs) // n)
    m = 0
    for b in engs[::step][:n]:
        m |= 1 << b
    return m


def _plan(T, topo):
    cores = list(T.cores)

    def near(c):
        return [d for d in cores if d != c and topo.chip(d) == topo.chip(c)]

    def far(c):
        return [d for d in cores if topo.chip(d) != topo.chip(c)]

    def gateway(ch):
        for c in cores:
            if topo.chip(c) == ch and all(topo.may_write(c, d) for d in far(c)):
                return c
        return None

    def off_mask(c):
        m = topo.mask(c, far(c)[0])
        for d in far(c):
            m &= topo.mask(c, d)
        return m

    def x_mask(c):
        on_chip = topo.mask(c, near(c)[0])
        if gateway(topo.chip(c)) == c:
            return on_chip
        return _pick(_engines(on_chip), 8)

    return near, far, gateway, off_mask, x_mask


def rank_program(g, core, T, topo):
    if T.rank_of(core) is None:
        return
    near, far, gateway, off_mask, x_mask = _plan(T, topo)
    S = T.sem
    nb = near(core)[0]
    gate = gateway(topo.chip(core)) == core
    fgate = gateway(topo.chip(far(core)[0]))

    def cols(buf, c, b=None):
        o = T.rank_of(c) * P
        if b is None:
            return buf[:, o:o + P]
        return buf[:, o + BLK[b][0]:o + BLK[b][1]]

    def blk(buf, b):
        return buf[:, BLK[b][0]:BLK[b][1]]

    pg = (T.pg0[:, 0:HB], T.pg1[:, 0:HB])
    py = (T.py0[:, 0:HB], T.py1[:, 0:HB])
    sg, sh, sfar = (S.g0, S.g1), (S.h0, S.h1), (S.far0, S.far1)
    sp, sy, sst = (S.p0, S.p1), (S.y0, S.y1), (S.st0, S.st1)
    n_far = _count(off_mask(fgate))

    if not gate:
        g.sync.dma_start(T.xd[:], T.x[:]).then_inc(S.ldxd, 16)
    g.sync.dma_start(T.xs[:], T.x[:]).then_inc(S.ldx, 16)
    g.sync.dma_start(T.xts[:], T.xt[:]).then_inc(S.ldxt, 16)

    left = 0
    nrid, npid, _ = topo.addr(nb)
    m = x_mask(core)
    if gate:
        g.wait_ge(S.ldx, 16)
        g.remote_dma(cols(T.px, core), T.xs[:], S.peer, S.left, npid, nrid, m)
    else:
        g.wait_ge(S.ldxd, 16)
        g.remote_dma(cols(T.px, core), T.xd[:], S.peer, S.left, npid, nrid, m)
    left += _count(m)
    if gate:
        mo = off_mask(core)
        for b in (0, 1):
            dsts = far(core) if b == 0 else far(core)[::-1]
            ids = []
            for d in dsts:
                rid, pid, _ = topo.addr(d)
                ids.append(DstId(rid=rid, pnc=pid))
            g.wait_ge(sh[b], 1)
            g.remote_dma_fused(
                [RemoteDMATransfer(dst_ids=ids, dma_engine_mask=mo, remote_sem=sfar[b],
                                   srcs=[blk(T.h, b)], dsts=[cols(T.hf, core, b) for _ in ids])],
                local_sem=S.left)
            left += _count(mo)
    g.wait_ge(S.left, left)

    t = g.tensor
    t.wait_ge(S.ldx, 16)
    for b in (0, 1):
        t.matmul(pg[b], T.xs[:], blk(T.xs, b), True, False)
    t.wait_ge(S.peer, _count(x_mask(nb)))
    for b in (0, 1):
        t.matmul(pg[b], cols(T.px, nb), cols(T.px, nb, b), False, True).then_inc(sg[b], 1)
    t.wait_ge(S.ldxt, 16)
    for b in (0, 1):
        t.wait_ge(sh[b], 1)
        t.matmul(py[b], T.xts[:], blk(T.h, b), True, False)
    for b in (0, 1):
        t.wait_ge(sfar[b], n_far)
        t.matmul(py[b], T.xts[:], cols(T.hf, fgate, b), False, True).then_inc(sp[b], 1)

    v = g.vector
    v.memset(T.cm[:], -0.5).then_inc(S.cst, 1)
    v.memset(T.cp[:], 1.5).then_inc(S.cst, 1)
    v.wait_ge(S.cst, 2)
    v.wait_ge(S.ldx, 16)
    v.tensor_tensor(T.x15[:], T.xs[:], T.cp[:], AluOpType.mult).then_inc(S.x15, 1)
    for b in (0, 1):
        v.wait_ge(sg[b], 1)
        v.tensor_tensor(blk(T.h, b), pg[b], T.cm[:], AluOpType.mult).then_inc(sh[b], 1)
    v.wait_ge(S.x15, 1)
    for b in (0, 1):
        v.wait_ge(sp[b], 1)
        v.tensor_tensor(blk(T.ys, b), py[b], blk(T.x15, b), AluOpType.add).then_inc(sy[b], 1)

    for q, b in ((g.scalar, 0), (g.sync, 1)):
        q.wait_ge(sy[b], 1)
        q.dma_start(blk(T.y, b), blk(T.ys, b)).then_inc(sst[b], 16)
        q.wait_ge(sst[b], 16)
